import numpy as np
import ml_dtypes


def mxq(x, axis, fmt="e4m3"):
    dtype, down = {"e4m3": (ml_dtypes.float8_e4m3fn, 7), "e5m2": (ml_dtypes.float8_e5m2, 14)}[fmt]
    v = np.moveaxis(np.asarray(x, np.float32).astype(ml_dtypes.bfloat16).astype(np.float64), axis, -1)
    blocks = v.reshape(v.shape[:-1] + (-1, 32))
    amax = np.abs(blocks).max(-1, keepdims=True)
    byte = np.maximum(np.where(amax > 0, np.frexp(amax)[1] - 1 + 127, 0) - down, 1)
    scale = np.exp2(byte - 127.0)
    codes = (blocks / scale).astype(np.float32).astype(dtype).astype(np.float64)
    return np.moveaxis((codes * scale).reshape(v.shape), -1, axis)


WIDE = False


def mx_kscale(k):
    if not WIDE:
        return np.ones(k)
    levels = np.array([10, -10, 5, -5, 0])
    if k % 512:
        return np.exp2(np.random.permutation(np.resize(levels, k // 32))).repeat(32)
    a = np.empty((k // 512, 16))
    for p in range(k // 512):
        a[p, :8] = np.random.permutation(np.resize(levels, 8))
        for g in range(8):
            far = levels[np.abs(levels - a[p, g]) >= 10]
            a[p, g + 8] = far[np.random.randint(len(far))]
    return np.exp2(a.ravel()).repeat(32)


def f64(x):
    return np.asarray(x).astype(np.float64)


def striped(idx):
    return np.tile(np.asarray(idx).reshape(-1, 16).T, (8, 1)).astype(np.uint16)


def unstriped(offs):
    return offs[:16].T.reshape(-1).astype(np.int64)


E2M1 = np.array([0.0, 0.5, 1.0, 1.5, 2.0, 3.0, 4.0, 6.0, -0.0, -0.5, -1.0, -1.5, -2.0, -3.0, -4.0, -6.0])


def pack_weight(w, fmt):
    k, n = w.shape
    w = f64(np.asarray(w, np.float32).astype(ml_dtypes.bfloat16)).reshape(k // 32, 32, n)
    amax = np.abs(w).max(1)
    if fmt == "e4m3":
        byte = np.frexp(amax)[1] - 1 + 127 - 7
    else:
        mant, ex = np.frexp(amax / 6.0)
        byte = np.where(mant > 0.5, ex, ex - 1) + 127
    byte = np.clip(np.where(amax > 0, byte, 1), 1, 254)
    scaled = (w * np.exp2(127.0 - byte)[:, None, :]).reshape(k, n).astype(np.float32)
    by_word = np.ascontiguousarray(scaled.reshape(k // 512, 128, 4, n).transpose(0, 1, 3, 2))
    if fmt == "e4m3":
        words = by_word.astype(ml_dtypes.float8_e4m3fn).view(np.uint8)
    else:
        c = by_word.astype(ml_dtypes.float4_e2m1fn).view(np.uint8) & 0xF
        words = (c[..., 0::2] | (c[..., 1::2] << 4)).reshape(k // 512, 128, 2 * n)
    return np.ascontiguousarray(words), np.ascontiguousarray(byte.astype(np.uint8).reshape(k // 512, 16, n))


def unpack_weight(words, scales, fmt):
    g, _, n = scales.shape
    words = np.ascontiguousarray(words).reshape(g, 128, n, -1)
    if fmt == "e4m3":
        vals = words.view(ml_dtypes.float8_e4m3fn).astype(np.float64)
    else:
        nib = np.empty((g, 128, n, 4), np.uint8)
        nib[..., 0::2] = words & 0xF
        nib[..., 1::2] = words >> 4
        vals = E2M1[nib]
    vals = vals * np.repeat(np.exp2(scales.astype(np.float64) - 127.0), 8, axis=1)[..., None]
    return vals.transpose(0, 1, 3, 2).reshape(g * 512, n)


D, E, T, I, Q = 512, 512, 2048, 512, 128


def setup_inputs():
    n = np.random.standard_normal
    idx = np.random.permutation(T)[:I]
    fd = mx_kscale(D)
    fe = mx_kscale(E)
    keysp = pack_weight(n((D, T)) / fd[:, None], "e4m3")
    valsp = pack_weight(n((E, T)) / fe[:, None], "e4m3")
    return {
        "query": (n((D, Q)) * 0.6 / np.sqrt(D) * fd[:, None]).astype(np.float32),
        "keys_words": keysp[0],
        "keys_scales": keysp[1],
        "pen": (np.random.uniform(0.2, 0.8, (Q, 1))).astype(np.float32),
        "gout": (n((E, Q)) * 1 / np.sqrt(E) * fe[:, None]).astype(np.float32),
        "vals_words": valsp[0],
        "vals_scales": valsp[1],
        "dquery": (n((D, Q)) * 1.0 / np.sqrt(D) * fd[:, None]).astype(np.float32),
        "base": (0.5 * n((Q, T))).astype(np.float32),
        "offs": striped(idx),
    }


def reference(query, keys_words, keys_scales, pen, gout, vals_words, vals_scales, dquery, base, offs):
    idx = unstriped(offs)
    keysu = unpack_weight(keys_words, keys_scales, "e4m3")
    valsu = unpack_weight(vals_words, vals_scales, "e4m3")
    queryq = mxq(f64(query), 0, "e4m3")
    keysidxg = keysu[:, idx]
    a = queryq.T @ keysidxg
    dqueryq = mxq(f64(dquery), 0, "e4m3")
    ta = dqueryq.T @ keysidxg
    p = np.exp(a - np.max(a, axis=1, keepdims=True))
    z = np.sum(p, axis=1, keepdims=True)
    goutq = mxq(f64(gout), 0, "e4m3")
    valsidxg = valsu[:, idx]
    c0 = goutq.T @ valsidxg
    m1 = np.sum(p * c0, axis=1, keepdims=True) / z
    dm1 = 1.0 + f64(pen) * m1 * 2.0
    dz = f64(pen) * (-1.0) * np.sum(p * np.square(c0), axis=1, keepdims=True) / np.square(z) * (-1.0) - dm1 * np.sum(p * c0, axis=1, keepdims=True) / np.square(z)
    dp = f64(pen) * (-1.0) / z * np.square(c0) + dm1 / z * c0 + dz
    tp = ta * p
    tz = np.sum(tp, axis=1, keepdims=True)
    tm1 = (np.sum(tp * c0, axis=1, keepdims=True) - tz * np.sum(p * c0, axis=1, keepdims=True) / z) / z
    tdm1 = tm1 * f64(pen) * 2.0
    tdz = (np.sum(tp * np.square(c0), axis=1, keepdims=True) * f64(pen) * (-1.0) - tz * z * 2.0 * f64(pen) * (-1.0) * np.sum(p * np.square(c0), axis=1, keepdims=True) / np.square(z)) / np.square(z) * (-1.0) - (tdm1 * np.sum(p * c0, axis=1, keepdims=True) + np.sum(tp * c0, axis=1, keepdims=True) * dm1 - tz * z * 2.0 * dm1 * np.sum(p * c0, axis=1, keepdims=True) / np.square(z)) / np.square(z)
    tdp = tz * f64(pen) * (-1.0) / np.square(z) * (-1.0) * np.square(c0) + (tdm1 - tz * dm1 / z) / z * c0 + tdz
    tda = tdp * p + tp * dp
    gs = tda * 512.0
    gf = np.zeros((Q, T))
    gf[:, idx] = gs
    y = f64(base) + gf
    return y

@@ -1,0 +1,161 @@
+from contextlib import ExitStack
+
+import concourse.mybir as mybir
+
+F32 = mybir.dt.float32
+BF16 = mybir.dt.bfloat16
+I32 = mybir.dt.int32
+U32 = mybir.dt.uint32
+U16 = mybir.dt.uint16
+U8 = mybir.dt.uint8
+FP8X4 = mybir.dt.float8_e4m3fn_x4
+ALU = mybir.AluOpType
+ACT = mybir.ActivationFunctionType
+
+P = 128
+PACK = 4
+K = 512
+T = 2048
+SLOTS = 512
+Q = 128
+GAIN = 512.0
+STORE_COLS = (256, 512, 512, 512, 256)
+
+FLOPS = 3 * 2 * K * Q * SLOTS
+
+
+def tile_attend_hvspreadpenalty_s_kernel(tc, query, keys_words, keys_scales, pen, gout, vals_words, vals_scales, dquery, base, offs, out):
+    nc = tc.nc
+    with ExitStack() as ctx:
+        keep = ctx.enter_context(tc.tile_pool(name="keep", bufs=1))
+        psum = ctx.enter_context(tc.psum_pool(name="psum", bufs=1))
+
+        def column(name, tag=None):
+            return keep.tile([P, 1], F32, name=name, tag=tag or name, align_bytes=64)
+
+        def slots(name, tag=None):
+            return keep.tile([P, SLOTS], F32, name=name, tag=tag or name, align_bytes=64)
+
+        def zeroed_scale_pool(name, engine):
+            pool_scales = keep.tile([P, T], U8, name=name, tag=name, align_bytes=64)
+            engine.memset(pool_scales[:].bitcast(I32), 0)
+            return pool_scales
+
+        def load_scales(pool_scales, scales):
+            for quad in range(4):
+                nc.sync.dma_start(pool_scales[32 * quad : 32 * quad + 4, :].bitcast(I32), scales[0, 4 * quad : 4 * quad + 4, :].bitcast(I32))
+
+        def load_words(name, words):
+            pool_words = keep.tile([P, T], I32, name=name, tag=name, align_bytes=64)
+            nc.sync.dma_start(pool_words[:], words[0].rearrange("p t r -> p (t r)").bitcast(I32))
+            return pool_words
+
+        def load_rows(name, rows):
+            raw = keep.tile([P, PACK, Q], F32, name=name)
+            nc.sync.dma_start(raw[:], rows.rearrange("(p j) q -> p j q", j=PACK))
+            return raw
+
+        def quantise(name, raw, cast):
+            grouped = keep.tile([P, Q, PACK], BF16, name=name + "_bf16", tag=name + "_bf16", align_bytes=64)
+            cast(grouped[:].rearrange("p (c i) j -> p c j i", i=4), raw[:].rearrange("p j (c i) -> p c j i", i=4))
+            codes = keep.tile([P, Q], U32, name=name + "_codes", align_bytes=64)
+            scales = keep.tile([P, Q], U8, name=name + "_scales", align_bytes=64)
+            nc.vector.quantize_mx(out=codes[:].bitcast(FP8X4), scales=scales[:], in_=grouped[:].rearrange("p q j -> p (q j)"))
+            return codes, scales
+
+        def gather(name, window, dtype):
+            picked = keep.tile([P, SLOTS], dtype, name=name, align_bytes=64)
+            nc.vector.tensor_copy(picked[:], window.indirect(offsets[:]))
+            return picked
+
+        def product(name, rows_mx, words, scales):
+            bank = psum.tile([Q, SLOTS], F32, name=name)
+            nc.tensor.matmul_mx(out=bank[:], lhsT=rows_mx[0][:].bitcast(FP8X4), lhsT_scale=rows_mx[1][:],
+                                rhs=words[:].bitcast(FP8X4), rhs_scale=scales[:], start=True, stop=True)
+            return bank
+
+        def fma(name, x, scale, bias):
+            y = column(name)
+            nc.scalar.activation(y[:], x[:], ACT.Identity, bias=bias, scale=scale)
+            return y
+
+        def weighted(name, x, scalar, op0, y, op1=ALU.mult, total=None, tag=None):
+            z = slots(name, tag)
+            nc.vector.scalar_tensor_tensor(z[:], x[:], scalar, y[:], op0, op1, accum_out=None if total is None else total[:])
+            return z
+
+        keys_scale_pool = zeroed_scale_pool("keys_scale_pool", nc.vector)
+        vals_scale_pool = zeroed_scale_pool("vals_scale_pool", nc.gpsimd)
+        offsets = keep.tile([P, SLOTS // 16], U16, name="offsets")
+        nc.sync.dma_start(offsets[:], offs)
+        penalty = column("penalty")
+        nc.sync.dma_start(penalty[:], pen)
+        query_raw = load_rows("query_raw", query)
+        load_scales(keys_scale_pool, keys_scales)
+        keys_pool = load_words("keys_pool", keys_words)
+        load_scales(vals_scale_pool, vals_scales)
+        gout_raw = load_rows("gout_raw", gout)
+        vals_pool = load_words("vals_pool", vals_words)
+        dquery_raw = load_rows("dquery_raw", dquery)
+        base_sb = keep.tile([P, T], F32, name="base_sb")
+        nc.sync.dma_start(base_sb[:], base)
+
+        warm = column("warm")
+        nc.vector.memset(warm[:], 0.0)
+        warm_out = column("warm_out")
+        nc.scalar.activation(warm_out[:], warm[:], ACT.Exp)
+        scattered = keep.tile([P, T], F32, name="scattered")
+        nc.vector.memset(scattered[:], 0.0)
+
+        keys_sc = gather("keys_sc", keys_scale_pool[:], U8)
+        query_mx = quantise("query", query_raw, nc.scalar.copy)
+        keys_codes = gather("keys_codes", keys_pool[:].bitcast(U32), U32)
+        a = product("a", query_mx, keys_codes, keys_sc)
+
+        vals_sc = gather("vals_sc", vals_scale_pool[:], U8)
+        neg_max = column("neg_max", "vals_scale_pool")
+        nc.vector.tensor_reduce(neg_max[:], a[:], mybir.AxisListType.X, ALU.max, negate=True)
+        p = slots("p")
+        z = column("z")
+        nc.scalar.activation(p[:], a[:], ACT.Exp, bias=neg_max[:], scale=1.0, accum_out=z[:])
+        gout_mx = quantise("gout", gout_raw, nc.scalar.copy)
+        vals_codes = gather("vals_codes", vals_pool[:].bitcast(U32), U32)
+        c = product("c", gout_mx, vals_codes, vals_sc)
+        dquery_mx = quantise("dquery", dquery_raw, nc.vector.tensor_copy)
+        ta = product("ta", dquery_mx, keys_codes, keys_sc)
+
+        pen_gain = fma("pen_gain", penalty, GAIN, 0.0)
+        pen_gain2 = fma("pen_gain2", penalty, 2.0 * GAIN, 0.0)
+        neg_pen_gain2 = fma("neg_pen_gain2", penalty, -2.0 * GAIN, 0.0)
+
+        inv_z = column("inv_z", "vals_pool")
+        nc.vector.reciprocal(inv_z[:], z[:])
+        w = slots("w")
+        nc.scalar.activation(w[:], p[:], ACT.Copy, scale=inv_z[:])
+
+        tb, m1, n1, g0, neg_k = (column(name) for name in ("tb", "m1", "n1", "g0", "neg_k"))
+        wc = weighted("wc", c, inv_z[:], ALU.mult, p, total=m1, tag="dquery_bf16")
+        neg_dm = fma("neg_dm", m1, neg_pen_gain2[:], -GAIN)
+        neg_lin = slots("neg_lin")
+        nc.scalar.activation(neg_lin[:], c[:], ACT.Identity, bias=neg_dm[:], scale=pen_gain[:])
+        wt = weighted("wt", ta, inv_z[:], ALU.mult, p, total=tb)
+        rc = weighted("rc", ta, tb[:], ALU.subtract, wc, total=n1)
+        weighted("wc_lin", wc, 1.0, ALU.mult, neg_lin, total=g0)
+        neg_x = weighted("neg_x", rc, 1.0, ALU.mult, neg_lin, total=neg_k)
+        tdm = fma("tdm", n1, pen_gain2[:], 0.0)
+        twc = slots("twc")
+        nc.scalar.activation(twc[:], wc[:], ACT.Copy, scale=tdm[:])
+        u1 = fma("u1", tdm, m1[:], 0.0)
+        u2 = fma("u2", g0, tb[:], u1[:])
+        hc = fma("hc", u2, -1.0, neg_k[:])
+        x3 = weighted("x3", wt, g0[:], ALU.mult, twc, op1=ALU.add)
+        x2 = weighted("x2", w, hc[:], ALU.mult, neg_x, op1=ALU.subtract)
+        nc.vector.tensor_tensor(scattered[:].indirect(offsets[:]), x3[:], x2[:], ALU.add)
+
+        start = 0
+        for piece, width in enumerate(STORE_COLS):
+            cols = slice(start, start + width)
+            result = keep.tile([P, width], F32, name="result%d" % piece)
+            nc.vector.tensor_tensor(result[:], scattered[:, cols], base_sb[:, cols], ALU.add)
+            nc.sync.dma_start(out[:, cols], result[:])
+            start = start + width

@@ -42,8 +42,8 @@ def tile_attend_hvspreadpenalty_s_kernel(tc, query, keys_words, keys_scales, pen
             return pool_scales
 
         def load_scales(pool_scales, scales):
-            for quad in range(4):
-                nc.sync.dma_start(pool_scales[32 * quad : 32 * quad + 4, :].bitcast(I32), scales[0, 4 * quad : 4 * quad + 4, :].bitcast(I32))
+            for row in range(4):
+                nc.sync.dma_start(pool_scales[row:P:32, :].bitcast(I32), scales[0, row:16:4, :].bitcast(I32))
 
         def load_words(name, words):
             pool_words = keep.tile([P, T], I32, name=name, tag=name, align_bytes=64)
@@ -51,7 +51,7 @@ def tile_attend_hvspreadpenalty_s_kernel(tc, query, keys_words, keys_scales, pen
             return pool_words
 
         def load_rows(name, rows):
-            raw = keep.tile([P, PACK, Q], F32, name=name)
+            raw = keep.tile([P, PACK, Q], F32, name=name, tag=name, align_bytes=64)
             nc.sync.dma_start(raw[:], rows.rearrange("(p j) q -> p j q", j=PACK))
             return raw
 
@@ -88,9 +88,9 @@ def tile_attend_hvspreadpenalty_s_kernel(tc, query, keys_words, keys_scales, pen
         vals_scale_pool = zeroed_scale_pool("vals_scale_pool", nc.gpsimd)
         offsets = keep.tile([P, SLOTS // 16], U16, name="offsets")
         nc.sync.dma_start(offsets[:], offs)
+        query_raw = load_rows("query_raw", query)
         penalty = column("penalty")
         nc.sync.dma_start(penalty[:], pen)
-        query_raw = load_rows("query_raw", query)
         load_scales(keys_scale_pool, keys_scales)
         keys_pool = load_words("keys_pool", keys_words)
         load_scales(vals_scale_pool, vals_scales)
@@ -119,9 +119,15 @@ def tile_attend_hvspreadpenalty_s_kernel(tc, query, keys_words, keys_scales, pen
         z = column("z")
         nc.scalar.activation(p[:], a[:], ACT.Exp, bias=neg_max[:], scale=1.0, accum_out=z[:])
         gout_mx = quantise("gout", gout_raw, nc.scalar.copy)
-        vals_codes = gather("vals_codes", vals_pool[:].bitcast(U32), U32)
-        c = product("c", gout_mx, vals_codes, vals_sc)
-        dquery_mx = quantise("dquery", dquery_raw, nc.vector.tensor_copy)
+        vals_codes = keep.tile([P, SLOTS], U32, name="vals_codes", align_bytes=64)
+        c = psum.tile([Q, SLOTS], F32, name="c")
+        for half in range(2):
+            cols = slice(half * SLOTS // 2, (half + 1) * SLOTS // 2)
+            entries = offsets[:, half * SLOTS // 32 : (half + 1) * SLOTS // 32]
+            nc.vector.tensor_copy(vals_codes[:, cols], vals_pool[:].bitcast(U32).indirect(entries))
+            nc.tensor.matmul_mx(out=c[:, cols], lhsT=gout_mx[0][:].bitcast(FP8X4), lhsT_scale=gout_mx[1][:],
+                                rhs=vals_codes[:, cols].bitcast(FP8X4), rhs_scale=vals_sc[:, cols], start=True, stop=True)
+        dquery_mx = quantise("dquery", dquery_raw, nc.scalar.copy)
         ta = product("ta", dquery_mx, keys_codes, keys_sc)
 
         pen_gain = fma("pen_gain", penalty, GAIN, 0.0)
@@ -130,7 +136,7 @@ def tile_attend_hvspreadpenalty_s_kernel(tc, query, keys_words, keys_scales, pen
 
         inv_z = column("inv_z", "vals_pool")
         nc.vector.reciprocal(inv_z[:], z[:])
-        w = slots("w")
+        w = slots("w", "dquery_raw")
         nc.scalar.activation(w[:], p[:], ACT.Copy, scale=inv_z[:])
 
         tb, m1, n1, g0, neg_k = (column(name) for name in ("tb", "m1", "n1", "g0", "neg_k"))

@@ -55,13 +55,15 @@ def tile_attend_hvspreadpenalty_s_kernel(tc, query, keys_words, keys_scales, pen
             nc.sync.dma_start(raw[:], rows.rearrange("(p j) q -> p j q", j=PACK))
             return raw
 
-        def quantise(name, raw, cast):
-            grouped = keep.tile([P, Q, PACK], BF16, name=name + "_bf16", tag=name + "_bf16", align_bytes=64)
-            cast(grouped[:].rearrange("p (c i) j -> p c j i", i=4), raw[:].rearrange("p j (c i) -> p c j i", i=4))
-            codes = keep.tile([P, Q], U32, name=name + "_codes", align_bytes=64)
-            scales = keep.tile([P, Q], U8, name=name + "_scales", align_bytes=64)
+        def quantise(name, raws):
+            width = Q * len(raws)
+            grouped = keep.tile([P, width, PACK], BF16, name=name + "_bf16", align_bytes=64)
+            for n, raw in enumerate(raws):
+                nc.scalar.copy(grouped[:, n * Q : (n + 1) * Q, :].rearrange("p (c i) j -> p c j i", i=4), raw[:].rearrange("p j (c i) -> p c j i", i=4))
+            codes = keep.tile([P, width], U32, name=name + "_codes", align_bytes=64)
+            scales = keep.tile([P, width], U8, name=name + "_scales", align_bytes=64)
             nc.vector.quantize_mx(out=codes[:].bitcast(FP8X4), scales=scales[:], in_=grouped[:].rearrange("p q j -> p (q j)"))
-            return codes, scales
+            return [(codes[:, n * Q : (n + 1) * Q], scales[:, n * Q : (n + 1) * Q]) for n in range(len(raws))]
 
         def gather(name, window, dtype):
             picked = keep.tile([P, SLOTS], dtype, name=name, align_bytes=64)
@@ -70,7 +72,7 @@ def tile_attend_hvspreadpenalty_s_kernel(tc, query, keys_words, keys_scales, pen
 
         def product(name, rows_mx, words, scales):
             bank = psum.tile([Q, SLOTS], F32, name=name)
-            nc.tensor.matmul_mx(out=bank[:], lhsT=rows_mx[0][:].bitcast(FP8X4), lhsT_scale=rows_mx[1][:],
+            nc.tensor.matmul_mx(out=bank[:], lhsT=rows_mx[0].bitcast(FP8X4), lhsT_scale=rows_mx[1],
                                 rhs=words[:].bitcast(FP8X4), rhs_scale=scales[:], start=True, stop=True)
             return bank
 
@@ -95,8 +97,8 @@ def tile_attend_hvspreadpenalty_s_kernel(tc, query, keys_words, keys_scales, pen
         keys_pool = load_words("keys_pool", keys_words)
         load_scales(vals_scale_pool, vals_scales)
         gout_raw = load_rows("gout_raw", gout)
-        vals_pool = load_words("vals_pool", vals_words)
         dquery_raw = load_rows("dquery_raw", dquery)
+        vals_pool = load_words("vals_pool", vals_words)
         base_sb = keep.tile([P, T], F32, name="base_sb")
         nc.sync.dma_start(base_sb[:], base)
 
@@ -108,27 +110,26 @@ def tile_attend_hvspreadpenalty_s_kernel(tc, query, keys_words, keys_scales, pen
         nc.vector.memset(scattered[:], 0.0)
 
         keys_sc = gather("keys_sc", keys_scale_pool[:], U8)
-        query_mx = quantise("query", query_raw, nc.scalar.copy)
+        (query_mx,) = quantise("query", [query_raw])
         keys_codes = gather("keys_codes", keys_pool[:].bitcast(U32), U32)
         a = product("a", query_mx, keys_codes, keys_sc)
 
         vals_sc = gather("vals_sc", vals_scale_pool[:], U8)
         neg_max = column("neg_max", "vals_scale_pool")
         nc.vector.tensor_reduce(neg_max[:], a[:], mybir.AxisListType.X, ALU.max, negate=True)
-        p = slots("p")
+        p = slots("p", "dquery_raw")
         z = column("z")
         nc.scalar.activation(p[:], a[:], ACT.Exp, bias=neg_max[:], scale=1.0, accum_out=z[:])
-        gout_mx = quantise("gout", gout_raw, nc.scalar.copy)
+        gout_mx, dquery_mx = quantise("late", [gout_raw, dquery_raw])
+        ta = product("ta", dquery_mx, keys_codes, keys_sc)
         vals_codes = keep.tile([P, SLOTS], U32, name="vals_codes", align_bytes=64)
         c = psum.tile([Q, SLOTS], F32, name="c")
         for half in range(2):
             cols = slice(half * SLOTS // 2, (half + 1) * SLOTS // 2)
             entries = offsets[:, half * SLOTS // 32 : (half + 1) * SLOTS // 32]
             nc.vector.tensor_copy(vals_codes[:, cols], vals_pool[:].bitcast(U32).indirect(entries))
-            nc.tensor.matmul_mx(out=c[:, cols], lhsT=gout_mx[0][:].bitcast(FP8X4), lhsT_scale=gout_mx[1][:],
+            nc.tensor.matmul_mx(out=c[:, cols], lhsT=gout_mx[0].bitcast(FP8X4), lhsT_scale=gout_mx[1],
                                 rhs=vals_codes[:, cols].bitcast(FP8X4), rhs_scale=vals_sc[:, cols], start=True, stop=True)
-        dquery_mx = quantise("dquery", dquery_raw, nc.scalar.copy)
-        ta = product("ta", dquery_mx, keys_codes, keys_sc)
 
         pen_gain = fma("pen_gain", penalty, GAIN, 0.0)
         pen_gain2 = fma("pen_gain2", penalty, 2.0 * GAIN, 0.0)
@@ -136,18 +137,19 @@ def tile_attend_hvspreadpenalty_s_kernel(tc, query, keys_words, keys_scales, pen
 
         inv_z = column("inv_z", "vals_pool")
         nc.vector.reciprocal(inv_z[:], z[:])
-        w = slots("w", "dquery_raw")
+        w = slots("w")
         nc.scalar.activation(w[:], p[:], ACT.Copy, scale=inv_z[:])
 
         tb, m1, n1, g0, neg_k = (column(name) for name in ("tb", "m1", "n1", "g0", "neg_k"))
-        wc = weighted("wc", c, inv_z[:], ALU.mult, p, total=m1, tag="dquery_bf16")
-        neg_dm = fma("neg_dm", m1, neg_pen_gain2[:], -GAIN)
-        neg_lin = slots("neg_lin")
-        nc.scalar.activation(neg_lin[:], c[:], ACT.Identity, bias=neg_dm[:], scale=pen_gain[:])
         wt = weighted("wt", ta, inv_z[:], ALU.mult, p, total=tb)
+        wc = weighted("wc", c, inv_z[:], ALU.mult, p, total=m1)
+        pen_c = slots("pen_c")
+        nc.scalar.activation(pen_c[:], c[:], ACT.Copy, scale=pen_gain[:])
+        neg_dm = column("neg_dm")
+        nc.gpsimd.tensor_scalar(neg_dm[:], m1[:], neg_pen_gain2[:], -GAIN, ALU.mult, ALU.add)
         rc = weighted("rc", ta, tb[:], ALU.subtract, wc, total=n1)
-        weighted("wc_lin", wc, 1.0, ALU.mult, neg_lin, total=g0)
-        neg_x = weighted("neg_x", rc, 1.0, ALU.mult, neg_lin, total=neg_k)
+        weighted("wc_lin", pen_c, neg_dm[:], ALU.add, wc, total=g0)
+        neg_x = weighted("neg_x", pen_c, neg_dm[:], ALU.add, rc, total=neg_k)
         tdm = fma("tdm", n1, pen_gain2[:], 0.0)
         twc = slots("twc")
         nc.scalar.activation(twc[:], wc[:], ACT.Copy, scale=tdm[:])

from contextlib import ExitStack

import concourse.mybir as mybir

F32 = mybir.dt.float32
BF16 = mybir.dt.bfloat16
I32 = mybir.dt.int32
U32 = mybir.dt.uint32
U16 = mybir.dt.uint16
U8 = mybir.dt.uint8
FP8X4 = mybir.dt.float8_e4m3fn_x4
ALU = mybir.AluOpType
ACT = mybir.ActivationFunctionType

P = 128
PACK = 4
K = 512
T = 2048
SLOTS = 512
Q = 128
GAIN = 512.0
STORE_COLS = (256, 512, 512, 512, 256)

FLOPS = 3 * 2 * K * Q * SLOTS


def tile_attend_hvspreadpenalty_s_kernel(tc, query, keys_words, keys_scales, pen, gout, vals_words, vals_scales, dquery, base, offs, out):
    nc = tc.nc
    with ExitStack() as ctx:
        keep = ctx.enter_context(tc.tile_pool(name="keep", bufs=1))
        psum = ctx.enter_context(tc.psum_pool(name="psum", bufs=1))

        def column(name, tag=None):
            return keep.tile([P, 1], F32, name=name, tag=tag or name, align_bytes=64)

        def slots(name, tag=None):
            return keep.tile([P, SLOTS], F32, name=name, tag=tag or name, align_bytes=64)

        def zeroed_scale_pool(name, engine):
            pool_scales = keep.tile([P, T], U8, name=name, tag=name, align_bytes=64)
            engine.memset(pool_scales[:].bitcast(I32), 0)
            return pool_scales

        def load_scales(pool_scales, scales):
            for row in range(4):
                nc.sync.dma_start(pool_scales[row:P:32, :].bitcast(I32), scales[0, row:16:4, :].bitcast(I32))

        def load_words(name, words):
            pool_words = keep.tile([P, T], I32, name=name, tag=name, align_bytes=64)
            nc.sync.dma_start(pool_words[:], words[0].rearrange("p t r -> p (t r)").bitcast(I32))
            return pool_words

        def load_rows(name, rows):
            raw = keep.tile([P, PACK, Q], F32, name=name, tag=name, align_bytes=64)
            nc.sync.dma_start(raw[:], rows.rearrange("(p j) q -> p j q", j=PACK))
            return raw

        def quantise(name, raws):
            width = Q * len(raws)
            grouped = keep.tile([P, width, PACK], BF16, name=name + "_bf16", align_bytes=64)
            for n, raw in enumerate(raws):
                nc.scalar.copy(grouped[:, n * Q : (n + 1) * Q, :].rearrange("p (c i) j -> p c j i", i=4), raw[:].rearrange("p j (c i) -> p c j i", i=4))
            codes = keep.tile([P, width], U32, name=name + "_codes", align_bytes=64)
            scales = keep.tile([P, width], U8, name=name + "_scales", align_bytes=64)
            nc.vector.quantize_mx(out=codes[:].bitcast(FP8X4), scales=scales[:], in_=grouped[:].rearrange("p q j -> p (q j)"))
            return [(codes[:, n * Q : (n + 1) * Q], scales[:, n * Q : (n + 1) * Q]) for n in range(len(raws))]

        def gather(name, window, dtype):
            picked = keep.tile([P, SLOTS], dtype, name=name, align_bytes=64)
            nc.vector.tensor_copy(picked[:], window.indirect(offsets[:]))
            return picked

        def product(name, rows_mx, words, scales):
            bank = psum.tile([Q, SLOTS], F32, name=name)
            nc.tensor.matmul_mx(out=bank[:], lhsT=rows_mx[0].bitcast(FP8X4), lhsT_scale=rows_mx[1],
                                rhs=words[:].bitcast(FP8X4), rhs_scale=scales[:], start=True, stop=True)
            return bank

        def fma(name, x, scale, bias):
            y = column(name)
            nc.scalar.activation(y[:], x[:], ACT.Identity, bias=bias, scale=scale)
            return y

        def weighted(name, x, scalar, op0, y, op1=ALU.mult, total=None, tag=None):
            z = slots(name, tag)
            nc.vector.scalar_tensor_tensor(z[:], x[:], scalar, y[:], op0, op1, accum_out=None if total is None else total[:])
            return z

        keys_scale_pool = zeroed_scale_pool("keys_scale_pool", nc.vector)
        vals_scale_pool = zeroed_scale_pool("vals_scale_pool", nc.gpsimd)
        offsets = keep.tile([P, SLOTS // 16], U16, name="offsets")
        nc.sync.dma_start(offsets[:], offs)
        query_raw = load_rows("query_raw", query)
        penalty = column("penalty")
        nc.sync.dma_start(penalty[:], pen)
        load_scales(keys_scale_pool, keys_scales)
        keys_pool = load_words("keys_pool", keys_words)
        load_scales(vals_scale_pool, vals_scales)
        gout_raw = load_rows("gout_raw", gout)
        dquery_raw = load_rows("dquery_raw", dquery)
        vals_pool = load_words("vals_pool", vals_words)
        base_sb = keep.tile([P, T], F32, name="base_sb")
        nc.sync.dma_start(base_sb[:], base)

        warm = column("warm")
        nc.vector.memset(warm[:], 0.0)
        warm_out = column("warm_out")
        nc.scalar.activation(warm_out[:], warm[:], ACT.Exp)
        scattered = keep.tile([P, T], F32, name="scattered")
        nc.vector.memset(scattered[:], 0.0)

        keys_sc = gather("keys_sc", keys_scale_pool[:], U8)
        (query_mx,) = quantise("query", [query_raw])
        keys_codes = gather("keys_codes", keys_pool[:].bitcast(U32), U32)
        a = product("a", query_mx, keys_codes, keys_sc)

        vals_sc = gather("vals_sc", vals_scale_pool[:], U8)
        neg_max = column("neg_max", "vals_scale_pool")
        nc.vector.tensor_reduce(neg_max[:], a[:], mybir.AxisListType.X, ALU.max, negate=True)
        p = slots("p", "dquery_raw")
        z = column("z")
        nc.scalar.activation(p[:], a[:], ACT.Exp, bias=neg_max[:], scale=1.0, accum_out=z[:])
        gout_mx, dquery_mx = quantise("late", [gout_raw, dquery_raw])
        ta = product("ta", dquery_mx, keys_codes, keys_sc)
        vals_codes = keep.tile([P, SLOTS], U32, name="vals_codes", align_bytes=64)
        c = psum.tile([Q, SLOTS], F32, name="c")
        for half in range(2):
            cols = slice(half * SLOTS // 2, (half + 1) * SLOTS // 2)
            entries = offsets[:, half * SLOTS // 32 : (half + 1) * SLOTS // 32]
            nc.vector.tensor_copy(vals_codes[:, cols], vals_pool[:].bitcast(U32).indirect(entries))
            nc.tensor.matmul_mx(out=c[:, cols], lhsT=gout_mx[0].bitcast(FP8X4), lhsT_scale=gout_mx[1],
                                rhs=vals_codes[:, cols].bitcast(FP8X4), rhs_scale=vals_sc[:, cols], start=True, stop=True)

        pen_gain = fma("pen_gain", penalty, GAIN, 0.0)
        pen_gain2 = fma("pen_gain2", penalty, 2.0 * GAIN, 0.0)
        neg_pen_gain2 = fma("neg_pen_gain2", penalty, -2.0 * GAIN, 0.0)

        inv_z = column("inv_z", "vals_pool")
        nc.vector.reciprocal(inv_z[:], z[:])
        w = slots("w")
        nc.scalar.activation(w[:], p[:], ACT.Copy, scale=inv_z[:])

        tb, m1, n1, g0, neg_k = (column(name) for name in ("tb", "m1", "n1", "g0", "neg_k"))
        wt = weighted("wt", ta, inv_z[:], ALU.mult, p, total=tb)
        wc = weighted("wc", c, inv_z[:], ALU.mult, p, total=m1)
        pen_c = slots("pen_c")
        nc.scalar.activation(pen_c[:], c[:], ACT.Copy, scale=pen_gain[:])
        neg_dm = column("neg_dm")
        nc.gpsimd.tensor_scalar(neg_dm[:], m1[:], neg_pen_gain2[:], -GAIN, ALU.mult, ALU.add)
        rc = weighted("rc", ta, tb[:], ALU.subtract, wc, total=n1)
        weighted("wc_lin", pen_c, neg_dm[:], ALU.add, wc, total=g0)
        neg_x = weighted("neg_x", pen_c, neg_dm[:], ALU.add, rc, total=neg_k)
        tdm = fma("tdm", n1, pen_gain2[:], 0.0)
        twc = slots("twc")
        nc.scalar.activation(twc[:], wc[:], ACT.Copy, scale=tdm[:])
        u1 = fma("u1", tdm, m1[:], 0.0)
        u2 = fma("u2", g0, tb[:], u1[:])
        hc = fma("hc", u2, -1.0, neg_k[:])
        x3 = weighted("x3", wt, g0[:], ALU.mult, twc, op1=ALU.add)
        x2 = weighted("x2", w, hc[:], ALU.mult, neg_x, op1=ALU.subtract)
        nc.vector.tensor_tensor(scattered[:].indirect(offsets[:]), x3[:], x2[:], ALU.add)

        start = 0
        for piece, width in enumerate(STORE_COLS):
            cols = slice(start, start + width)
            result = keep.tile([P, width], F32, name="result%d" % piece)
            nc.vector.tensor_tensor(result[:], scattered[:, cols], base_sb[:, cols], ALU.add)
            nc.sync.dma_start(out[:, cols], result[:])
            start = start + width
